import numpy as np
import ml_dtypes


def mxq(x, axis, fmt="e4m3"):
    dtype, down = {"e4m3": (ml_dtypes.float8_e4m3fn, 7), "e5m2": (ml_dtypes.float8_e5m2, 14)}[fmt]
    v = np.moveaxis(np.asarray(x, np.float32).astype(ml_dtypes.bfloat16).astype(np.float64), axis, -1)
    blocks = v.reshape(v.shape[:-1] + (-1, 32))
    amax = np.abs(blocks).max(-1, keepdims=True)
    byte = np.maximum(np.where(amax > 0, np.frexp(amax)[1] - 1 + 127, 0) - down, 1)
    scale = np.exp2(byte - 127.0)
    codes = (blocks / scale).astype(np.float32).astype(dtype).astype(np.float64)
    return np.moveaxis((codes * scale).reshape(v.shape), -1, axis)


WIDE = False


def mx_kscale(k):
    if not WIDE:
        return np.ones(k)
    levels = np.array([30, -30])
    if k % 512:
        return np.exp2(np.random.permutation(np.resize(levels, k // 32))).repeat(32)
    a = np.empty((k // 512, 16))
    for p in range(k // 512):
        a[p, :8] = np.random.permutation(np.resize(levels, 8))
        for g in range(8):
            far = levels[np.abs(levels - a[p, g]) >= 10]
            a[p, g + 8] = far[np.random.randint(len(far))]
    return np.exp2(a.ravel()).repeat(32)


def f64(x):
    return np.asarray(x).astype(np.float64)


def striped(idx):
    return np.tile(np.asarray(idx).reshape(-1, 16).T, (8, 1)).astype(np.uint16)


def unstriped(offs):
    return offs[:16].T.reshape(-1).astype(np.int64)


E2M1 = np.array([0.0, 0.5, 1.0, 1.5, 2.0, 3.0, 4.0, 6.0, -0.0, -0.5, -1.0, -1.5, -2.0, -3.0, -4.0, -6.0])


def pack_weight(w, fmt):
    k, n = w.shape
    w = f64(np.asarray(w, np.float32).astype(ml_dtypes.bfloat16)).reshape(k // 32, 32, n)
    amax = np.abs(w).max(1)
    if fmt in ("e4m3", "e5m2"):
        byte = np.frexp(amax)[1] - 1 + 127 - (7 if fmt == "e4m3" else 14)
    else:
        mant, ex = np.frexp(amax / 6.0)
        byte = np.where(mant > 0.5, ex, ex - 1) + 127
    byte = np.clip(np.where(amax > 0, byte, 1), 1, 254)
    scaled = (w * np.exp2(127.0 - byte)[:, None, :]).reshape(k, n).astype(np.float32)
    by_word = np.ascontiguousarray(scaled.reshape(k // 512, 128, 4, n).transpose(0, 1, 3, 2))
    if fmt in ("e4m3", "e5m2"):
        words = by_word.astype(ml_dtypes.float8_e4m3fn if fmt == "e4m3" else ml_dtypes.float8_e5m2).view(np.uint8)
    else:
        c = by_word.astype(ml_dtypes.float4_e2m1fn).view(np.uint8) & 0xF
        words = (c[..., 0::2] | (c[..., 1::2] << 4)).reshape(k // 512, 128, 2 * n)
    return np.ascontiguousarray(words), np.ascontiguousarray(byte.astype(np.uint8).reshape(k // 512, 16, n))


def unpack_weight(words, scales, fmt):
    g, _, n = scales.shape
    words = np.ascontiguousarray(words).reshape(g, 128, n, -1)
    if fmt in ("e4m3", "e5m2"):
        vals = words.view(ml_dtypes.float8_e4m3fn if fmt == "e4m3" else ml_dtypes.float8_e5m2).astype(np.float64)
    else:
        nib = np.empty((g, 128, n, 4), np.uint8)
        nib[..., 0::2] = words & 0xF
        nib[..., 1::2] = words >> 4
        vals = E2M1[nib]
    vals = vals * np.repeat(np.exp2(scales.astype(np.float64) - 127.0), 8, axis=1)[..., None]
    return vals.transpose(0, 1, 3, 2).reshape(g * 512, n)


K, F, T, Z, J, R, N, C, O = 512, 512, 1024, 1024, 256, 512, 256, 512, 128


def setup_inputs():
    n = np.random.standard_normal
    idx = np.random.permutation(T)[:J]
    idx2 = np.random.permutation(Z)[:J]
    idx3 = np.random.permutation(C)[:J]
    idx4 = np.random.permutation(C)[:C]
    idx5 = np.random.permutation(C)[:O]
    idx6 = np.random.permutation(J)[:O]
    fk = mx_kscale(K)
    fr = mx_kscale(R)
    ff = mx_kscale(F)
    xtp = pack_weight(n((K, T)) / fk[:, None], "e5m2")
    wp = pack_weight(n((K, R)) * 1 / np.sqrt(K) * fk[:, None] * fr, "e2m1")
    xop = pack_weight(n((F, Z)) / ff[:, None], "e4m3")
    w0p = pack_weight(n((F, R)) * 1 / np.sqrt(F) * ff[:, None] * fr, "e2m1")
    wbp = pack_weight(n((R, N)) * 1 / np.sqrt(R) / fr[:, None], "e2m1")
    wcp = pack_weight(n((R, N)) * 1 / np.sqrt(R) / fr[:, None], "e4m3")
    return {
        "xt_words": xtp[0],
        "xt_scales": xtp[1],
        "w_words": wp[0],
        "w_scales": wp[1],
        "xo_words": xop[0],
        "xo_scales": xop[1],
        "w0_words": w0p[0],
        "w0_scales": w0p[1],
        "wb_words": wbp[0],
        "wb_scales": wbp[1],
        "wc_words": wcp[0],
        "wc_scales": wcp[1],
        "offs": striped(idx),
        "offs2": striped(idx2),
        "offs3": striped(idx3),
        "offs4": striped(idx4),
        "offs5": striped(idx5),
        "offs6": striped(idx6),
    }


def reference(xt_words, xt_scales, w_words, w_scales, xo_words, xo_scales, w0_words, w0_scales, wb_words, wb_scales, wc_words, wc_scales, offs, offs2, offs3, offs4, offs5, offs6):
    idx = unstriped(offs)
    idx2 = unstriped(offs2)
    idx3 = unstriped(offs3)
    idx4 = unstriped(offs4)
    idx5 = unstriped(offs5)
    idx6 = unstriped(offs6)
    xtu = unpack_weight(xt_words, xt_scales, "e5m2")
    wu = unpack_weight(w_words, w_scales, "e2m1")
    xou = unpack_weight(xo_words, xo_scales, "e4m3")
    w0u = unpack_weight(w0_words, w0_scales, "e2m1")
    wbu = unpack_weight(wb_words, wb_scales, "e2m1")
    wcu = unpack_weight(wc_words, wc_scales, "e4m3")
    xtidxg = xtu[:, idx]
    xoidx2g = xou[:, idx2]
    a = wu.T @ xtidxg + w0u.T @ xoidx2g
    hid = np.maximum(a, 0.0)
    hidq = mxq(hid, 0, "e4m3")
    p = wbu.T @ hidq
    q = wcu.T @ hidq
    pw = np.zeros((N, C))
    pw[:, idx3] = p
    pg = pw - pw[:, idx4]
    y = np.maximum(pg[:, idx5], q[:, idx6])
    return y

@@ -1,0 +1,238 @@
+from contextlib import ExitStack
+
+import concourse.mybir as mybir
+
+K, F, T, Z, J, R, N, C, O = 512, 512, 1024, 1024, 256, 512, 256, 512, 128
+FLOPS = 2 * (K * R * J + F * R * J + 2 * R * N * J)
+
+F32 = mybir.dt.float32
+BF16 = mybir.dt.bfloat16
+I32 = mybir.dt.int32
+U32 = mybir.dt.uint32
+U16 = mybir.dt.uint16
+U8 = mybir.dt.uint8
+E4M3 = mybir.dt.float8_e4m3fn_x4
+E5M2 = mybir.dt.float8_e5m2_x4
+E2M1 = mybir.dt.float4_e2m1fn_x4
+ACT = mybir.ActivationFunctionType
+ALU = mybir.AluOpType
+
+P = 128
+H = 128
+
+
+def tile_list_chained_bank_kernel(
+    tc, xt_words, xt_scales, w_words, w_scales, xo_words, xo_scales, w0_words, w0_scales,
+    wb_words, wb_scales, wc_words, wc_scales, offs, offs2, offs3, offs4, offs5, offs6, out,
+):
+    nc = tc.nc
+    with ExitStack() as ctx:
+        sb = ctx.enter_context(tc.tile_pool(name="sb", bufs=1))
+        ps = ctx.enter_context(tc.psum_pool(name="ps", bufs=1))
+
+        def tile(name, shape, dtype, tag=None):
+            return sb.tile(shape, dtype, name=name, tag=tag or name, align_bytes=64)
+
+        l1 = tile("l1", [P, 16], U16)
+        l2 = tile("l2", [P, 16], U16)
+        l3 = tile("l3", [P, 16], U16)
+        l4 = tile("l4", [P, 32], U16)
+        l5 = tile("l5", [P, 8], U16)
+        l6 = tile("l6", [P, 8], U16)
+        xt_w = tile("xt_w", [P, T], U32)
+        xo_w = tile("xo_w", [P, Z], U32)
+        xt_s = tile("xt_s", [P, 2 * T], U8)
+        xo_s = tile("xo_s", [P, 2 * Z], U8)
+        w_raw = tile("w_raw", [P, 2 * R], U8)
+        w0_raw = tile("w0_raw", [P, 2 * R], U8)
+        w_dealt = tile("w_dealt", [P, 2 * R], U8)
+        w0_dealt = tile("w0_dealt", [P, 2 * R], U8)
+        ws_raw = tile("ws_raw", [P, 2 * 2 * R], U8)
+        ws_dealt = tile("ws_dealt", [P, R], U8)
+        w0s_dealt = tile("w0s_dealt", [P, R], U8)
+        wb_w = tile("wb_w", [P, 2 * N], U8)
+        wc_w = tile("wc_w", [P, N], U32)
+        wbc_s = tile("wbc_s", [P, 2 * 2 * N], U8)
+        pw = [tile("pw%d" % n, [P, C], F32) for n in range(2)]
+
+        nc.vector.memset(xt_s[:].bitcast(I32), 0)
+        nc.vector.memset(ws_raw[:].bitcast(I32), 0)
+        nc.vector.memset(xo_s[:].bitcast(I32), 0)
+        nc.vector.memset(wbc_s[:].bitcast(I32), 0)
+        for n in range(2):
+            nc.vector.memset(pw[n][:], 0.0)
+
+        def words4(ap):
+            return ap[0].rearrange("p n t -> p (n t)").bitcast(I32)
+
+        def rows_hl(ap, l):
+            return ap[0].bitcast(I32).rearrange("(h l r) n -> l r h n", h=2, l=2)[l]
+
+        ws_words = ws_raw[:].bitcast(I32).rearrange("p (h a n) -> p h a n", h=2, a=2)
+        xt_s_words = xt_s[:].bitcast(I32).rearrange("p (h n) -> p h n", h=2)
+        xo_s_words = xo_s[:].bitcast(I32).rearrange("p (h n) -> p h n", h=2)
+        wbc_words = wbc_s[:].bitcast(I32).rearrange("p (h a n) -> p h a n", h=2, a=2)
+
+        nc.sync.dma_start(l1[:], offs)
+        nc.sync.dma_start(l2[:], offs2)
+        for l in range(2):
+            nc.scalar.dma_start(xt_s_words[64 + 32 * l : 68 + 32 * l], rows_hl(xt_scales, l))
+        for a, scales in enumerate((w_scales, w0_scales)):
+            for l in range(2):
+                nc.scalar.dma_start(ws_words[32 * l : 32 * l + 4, :, a, :], rows_hl(scales, l))
+        for l in range(2):
+            nc.scalar.dma_start(xo_s_words[64 + 32 * l : 68 + 32 * l], rows_hl(xo_scales, l))
+        nc.sync.dma_start(xt_w[:].bitcast(I32), words4(xt_words))
+        nc.sync.dma_start(w_raw[:].bitcast(I32), w_words[0].bitcast(I32))
+        nc.sync.dma_start(w0_raw[:].bitcast(I32), w0_words[0].bitcast(I32))
+        nc.sync.dma_start(xo_w[:].bitcast(I32), words4(xo_words))
+        nc.sync.dma_start(wb_w[:].bitcast(I32), wb_words[0].bitcast(I32))
+        for l in range(2):
+            nc.sync.dma_start(wbc_words[32 * l : 32 * l + 4, :, 0, :], rows_hl(wb_scales, l))
+        nc.sync.dma_start(l3[:], offs3)
+        nc.sync.dma_start(wc_w[:].bitcast(I32), words4(wc_words))
+        for l in range(2):
+            nc.sync.dma_start(wbc_words[32 * l : 32 * l + 4, :, 1, :], rows_hl(wc_scales, l))
+        nc.sync.dma_start(l4[:], offs4)
+        nc.sync.dma_start(l6[:], offs6)
+        nc.sync.dma_start(l5[:], offs5)
+
+        def deal(dst, src, run):
+            return (dst.rearrange("p (t c i) -> p c t i", t=4, i=run), src.rearrange("p (c i t) -> p c t i", t=4, i=run))
+
+        for dst, src in ((w_dealt, w_raw), (w0_dealt, w0_raw)):
+            o_ap, i_ap = deal(dst[:].bitcast(U16), src[:].bitcast(U16), 8)
+            nc.scalar.copy(o_ap, i_ap)
+
+        def spread(plane, staged):
+            nc.vector.tensor_copy(plane[0:64, :].bitcast(I32), staged[64:128, 0, :])
+            nc.vector.tensor_copy(plane[64:128, :].bitcast(I32), staged[64:128, 1, :])
+
+        def deal_scales(dst, a):
+            nc.vector.tensor_copy(ws_words[64:128, 0, a, :], ws_words[0:64, 1, a, :])
+            o_ap, i_ap = deal(dst[:], ws_raw[:, a * R : (a + 1) * R], 16)
+            nc.vector.tensor_copy(o_ap, i_ap)
+
+        xt_plane = tile("xt_plane", [P, T], U8)
+        xo_plane = tile("xo_plane", [P, Z], U8)
+        xtg_w = tile("xtg_w", [P, J], U32)
+        xtg_s = tile("xtg_s", [P, J], U8)
+        xog_s = tile("xog_s", [P, J], U8)
+        spread(xt_plane, xt_s_words)
+        nc.vector.tensor_copy(xtg_s[:], xt_plane[:].indirect(l1[:]))
+        deal_scales(ws_dealt, 0)
+        nc.vector.tensor_copy(xtg_w[:], xt_w[:].indirect(l1[:]))
+
+        acc = [ps.tile([P, 4, H], F32, name="acc%d" % h) for h in range(2)]
+        for h in range(2):
+            for t in range(4):
+                nc.tensor.matmul_mx(
+                    acc[h][:, t, :],
+                    lhsT=w_dealt[:, 256 * t : 256 * (t + 1)].bitcast(E2M1),
+                    lhsT_scale=ws_dealt[:, 128 * t : 128 * (t + 1)],
+                    rhs=xtg_w[:, H * h : H * (h + 1)].bitcast(E5M2),
+                    rhs_scale=xtg_s[:, H * h : H * (h + 1)],
+                    start=(t == 0),
+                    stop=False,
+                )
+
+        deal_scales(w0s_dealt, 1)
+        spread(xo_plane, xo_s_words)
+        nc.vector.tensor_copy(xog_s[:], xo_plane[:].indirect(l2[:]))
+        xog_w = tile("xog_w", [P, J], U32, tag="xo_s")
+
+        hid = [tile("hid%d" % h, [P, H, 4], BF16) for h in range(2)]
+        for h in range(2):
+            nc.vector.tensor_copy(xog_w[:, H * h : H * (h + 1)], xo_w[:].indirect(l2[:, 8 * h : 8 * (h + 1)]))
+        for h in range(2):
+            for t in range(4):
+                nc.tensor.matmul_mx(
+                    acc[h][:, t, :],
+                    lhsT=w0_dealt[:, 256 * t : 256 * (t + 1)].bitcast(E2M1),
+                    lhsT_scale=w0s_dealt[:, 128 * t : 128 * (t + 1)],
+                    rhs=xog_w[:, H * h : H * (h + 1)].bitcast(E4M3),
+                    rhs_scale=xog_s[:, H * h : H * (h + 1)],
+                    start=False,
+                    stop=(t == 3),
+                )
+            nc.scalar.activation(hid[h][:], acc[h][:].rearrange("p t j -> p j t"), ACT.Relu)
+
+        wbc_plane = tile("wbc_plane", [P, 2 * N], U8, tag="xo_w")
+        wbc_flat = wbc_s[:].bitcast(I32)
+        nc.vector.tensor_copy(wbc_plane[0:64, :].bitcast(I32), wbc_flat[0:64, 0:128])
+        nc.vector.tensor_copy(wbc_plane[64:128, :].bitcast(I32), wbc_flat[0:64, 128:256])
+
+        hq_w = tile("hq_w", [P, J], U32, tag="wbc_s")
+        hq_s = tile("hq_s", [P, J], U8)
+        p_ps = [[ps.tile([P, H], F32, name="p_ps%d%d" % (h, n)) for n in range(2)] for h in range(2)]
+        q_ps = [ps.tile([P, J], F32, name="q_ps%d" % n) for n in range(2)]
+        for h in range(2):
+            cols = slice(H * h, H * (h + 1))
+            nc.vector.quantize_mx(
+                out=hq_w[:, cols].bitcast(E4M3), scales=hq_s[:, cols], in_=hid[h][:].rearrange("p j t -> p (j t)")
+            )
+            for n in range(2):
+                nc.tensor.matmul_mx(
+                    p_ps[h][n][:],
+                    lhsT=wb_w[:, 256 * n : 256 * (n + 1)].bitcast(E2M1),
+                    lhsT_scale=wbc_plane[:, 128 * n : 128 * (n + 1)],
+                    rhs=hq_w[:, cols].bitcast(E4M3),
+                    rhs_scale=hq_s[:, cols],
+                    start=True,
+                    stop=True,
+                )
+        for n in range(2):
+            nc.tensor.matmul_mx(
+                q_ps[n][:],
+                lhsT=wc_w[:, 128 * n : 128 * (n + 1)].bitcast(E4M3),
+                lhsT_scale=wbc_plane[:, N + 128 * n : N + 128 * (n + 1)],
+                rhs=hq_w[:].bitcast(E4M3),
+                rhs_scale=hq_s[:],
+                start=True,
+                stop=True,
+            )
+        p_sb = [
+            [tile("p_sb00", [P, H], F32, tag="hid1"), tile("p_sb01", [P, H], F32)],
+            [tile("p_sb10", [P, H], F32), tile("p_sb11", [P, H], F32)],
+        ]
+        pg = [tile("pg%d" % n, [P, C], F32) for n in range(2)]
+        pick_p = [tile("pick_p%d" % n, [P, O], F32) for n in range(2)]
+        pick_q = [tile("pick_q%d" % n, [P, O], F32) for n in range(2)]
+        y = [tile("y%d" % n, [P, O], F32) for n in range(2)]
+
+        def move(n, dst, src):
+            if n == 0:
+                nc.vector.tensor_copy(dst, src)
+            else:
+                nc.scalar.activation(dst, src, ACT.Copy)
+
+        for n in range(2):
+            move(n, p_sb[0][n][:], p_ps[0][n][:])
+            move(n, pw[n][:].indirect(l3[:, 0:8]), p_sb[0][n][:])
+        q_sb = [tile("q_sb0", [P, J], F32, tag="hid1"), tile("q_sb1", [P, J], F32, tag="p_sb01")]
+        for n in range(2):
+            move(n, p_sb[1][n][:], p_ps[1][n][:])
+            move(n, q_sb[n][:], q_ps[n][:])
+            move(n, pw[n][:].indirect(l3[:, 8:16]), p_sb[1][n][:])
+            move(n, pick_q[n][:], q_sb[n][:].indirect(l6[:]))
+
+        moved = [tile("moved%d" % n, [P, C], F32) for n in range(2)]
+
+        def fetch(engine, n, c0, c1):
+            move(engine, moved[n][:, c0:c1], pw[n][:].indirect(l4[:, c0 // 16 : c1 // 16]))
+
+        def sub(n, c0, c1):
+            nc.vector.tensor_tensor(pg[n][:, c0:c1], pw[n][:, c0:c1], moved[n][:, c0:c1], ALU.subtract)
+
+        fetch(0, 0, 0, 256)
+        fetch(1, 0, 256, 512)
+        fetch(0, 1, 384, 512)
+        fetch(1, 1, 0, 256)
+        fetch(1, 1, 256, 384)
+        sub(0, 0, 512)
+        sub(1, 0, 256)
+        sub(1, 256, 512)
+        for n in range(2):
+            move(1, pick_p[n][:], pg[n][:].indirect(l5[:]))
+            nc.vector.tensor_tensor(y[n][:], pick_p[n][:], pick_q[n][:], ALU.max)
+            nc.sync.dma_start(out[n * P : (n + 1) * P, :], y[n][:])

@@ -47,54 +47,53 @@ def tile_list_chained_bank_kernel(
         w0_raw = tile("w0_raw", [P, 2 * R], U8)
         w_dealt = tile("w_dealt", [P, 2 * R], U8)
         w0_dealt = tile("w0_dealt", [P, 2 * R], U8)
-        ws_raw = tile("ws_raw", [P, 2 * 2 * R], U8)
+        ws_raw = tile("ws_raw", [P, 4 * 2 * R], U8)
         ws_dealt = tile("ws_dealt", [P, R], U8)
         w0s_dealt = tile("w0s_dealt", [P, R], U8)
-        wb_w = tile("wb_w", [P, 2 * N], U8)
-        wc_w = tile("wc_w", [P, N], U32)
-        wbc_s = tile("wbc_s", [P, 2 * 2 * N], U8)
+        wbc_s = tile("wbc_s", [P, 4 * 2 * N], U8)
         pw = [tile("pw%d" % n, [P, C], F32) for n in range(2)]
 
-        nc.vector.memset(xt_s[:].bitcast(I32), 0)
-        nc.vector.memset(ws_raw[:].bitcast(I32), 0)
-        nc.vector.memset(xo_s[:].bitcast(I32), 0)
-        nc.vector.memset(wbc_s[:].bitcast(I32), 0)
-        for n in range(2):
-            nc.vector.memset(pw[n][:], 0.0)
+        ws_plane = tile("ws_plane", [P, 2 * R], U8)
+
+        nc.vector.memset(xt_s[:, 0:T].bitcast(I32), 0)
+        nc.gpsimd.memset(xt_s[:, T : 2 * T].bitcast(I32), 0)
+        nc.vector.memset(xo_s[:, 0:Z].bitcast(I32), 0)
+        nc.gpsimd.memset(xo_s[:, Z : 2 * Z].bitcast(I32), 0)
+        nc.vector.memset(ws_plane[:].bitcast(I32), 0)
+        nc.vector.memset(pw[0][:], 0.0)
+        nc.gpsimd.memset(pw[1][:], 0.0)
 
         def words4(ap):
             return ap[0].rearrange("p n t -> p (n t)").bitcast(I32)
 
+        def rows_q(ap):
+            return ap[0].bitcast(I32).rearrange("(q r) n -> r q n", r=4)
+
         def rows_hl(ap, l):
             return ap[0].bitcast(I32).rearrange("(h l r) n -> l r h n", h=2, l=2)[l]
 
-        ws_words = ws_raw[:].bitcast(I32).rearrange("p (h a n) -> p h a n", h=2, a=2)
+        ws_words = ws_raw[:].bitcast(I32).rearrange("p (q a n) -> p q a n", q=4, a=2)
         xt_s_words = xt_s[:].bitcast(I32).rearrange("p (h n) -> p h n", h=2)
         xo_s_words = xo_s[:].bitcast(I32).rearrange("p (h n) -> p h n", h=2)
-        wbc_words = wbc_s[:].bitcast(I32).rearrange("p (h a n) -> p h a n", h=2, a=2)
+        wbc_words = wbc_s[:].bitcast(I32).rearrange("p (q a n) -> p q a n", q=4, a=2)
 
         nc.sync.dma_start(l1[:], offs)
-        nc.sync.dma_start(l2[:], offs2)
-        for l in range(2):
-            nc.scalar.dma_start(xt_s_words[64 + 32 * l : 68 + 32 * l], rows_hl(xt_scales, l))
         for a, scales in enumerate((w_scales, w0_scales)):
-            for l in range(2):
-                nc.scalar.dma_start(ws_words[32 * l : 32 * l + 4, :, a, :], rows_hl(scales, l))
+            nc.scalar.dma_start(ws_words[0:4, :, a, :], rows_q(scales))
         for l in range(2):
-            nc.scalar.dma_start(xo_s_words[64 + 32 * l : 68 + 32 * l], rows_hl(xo_scales, l))
+            nc.sync.dma_start(xt_s_words[64 + 32 * l : 68 + 32 * l], rows_hl(xt_scales, l))
+        nc.scalar.dma_start(w_raw[:].bitcast(I32), w_words[0].bitcast(I32))
         nc.sync.dma_start(xt_w[:].bitcast(I32), words4(xt_words))
-        nc.sync.dma_start(w_raw[:].bitcast(I32), w_words[0].bitcast(I32))
+        nc.scalar.dma_start(xo_s_words[64:68], rows_hl(xo_scales, 0))
+        nc.sync.dma_start(l2[:], offs2)
+        nc.sync.dma_start(xo_s_words[96:100], rows_hl(xo_scales, 1))
         nc.sync.dma_start(w0_raw[:].bitcast(I32), w0_words[0].bitcast(I32))
         nc.sync.dma_start(xo_w[:].bitcast(I32), words4(xo_words))
-        nc.sync.dma_start(wb_w[:].bitcast(I32), wb_words[0].bitcast(I32))
-        for l in range(2):
-            nc.sync.dma_start(wbc_words[32 * l : 32 * l + 4, :, 0, :], rows_hl(wb_scales, l))
+        for a, scales in enumerate((wb_scales, wc_scales)):
+            nc.sync.dma_start(wbc_words[0:4, :, a, :], rows_q(scales))
         nc.sync.dma_start(l3[:], offs3)
-        nc.sync.dma_start(wc_w[:].bitcast(I32), words4(wc_words))
-        for l in range(2):
-            nc.sync.dma_start(wbc_words[32 * l : 32 * l + 4, :, 1, :], rows_hl(wc_scales, l))
-        nc.sync.dma_start(l4[:], offs4)
         nc.sync.dma_start(l6[:], offs6)
+        nc.sync.dma_start(l4[:], offs4)
         nc.sync.dma_start(l5[:], offs5)
 
         def deal(dst, src, run):
@@ -103,14 +102,15 @@ def tile_list_chained_bank_kernel(
         for dst, src in ((w_dealt, w_raw), (w0_dealt, w0_raw)):
             o_ap, i_ap = deal(dst[:].bitcast(U16), src[:].bitcast(U16), 8)
             nc.scalar.copy(o_ap, i_ap)
+        wb_w = tile("wb_w", [P, 2 * N], U8, tag="w_raw")
+        nc.scalar.dma_start(wb_w[:].bitcast(I32), wb_words[0].bitcast(I32))
 
         def spread(plane, staged):
             nc.vector.tensor_copy(plane[0:64, :].bitcast(I32), staged[64:128, 0, :])
             nc.vector.tensor_copy(plane[64:128, :].bitcast(I32), staged[64:128, 1, :])
 
         def deal_scales(dst, a):
-            nc.vector.tensor_copy(ws_words[64:128, 0, a, :], ws_words[0:64, 1, a, :])
-            o_ap, i_ap = deal(dst[:], ws_raw[:, a * R : (a + 1) * R], 16)
+            o_ap, i_ap = deal(dst[:], ws_plane[:, a * R : (a + 1) * R], 16)
             nc.vector.tensor_copy(o_ap, i_ap)
 
         xt_plane = tile("xt_plane", [P, T], U8)
@@ -118,10 +118,16 @@ def tile_list_chained_bank_kernel(
         xtg_w = tile("xtg_w", [P, J], U32)
         xtg_s = tile("xtg_s", [P, J], U8)
         xog_s = tile("xog_s", [P, J], U8)
+        ws_flat = ws_raw[:].bitcast(I32)
+        quarter = 2 * R // 4
+        for q in range(4):
+            nc.vector.tensor_copy(ws_plane[32 * q : 32 * q + 4, :].bitcast(I32), ws_flat[0:4, q * quarter : (q + 1) * quarter])
+        deal_scales(ws_dealt, 0)
         spread(xt_plane, xt_s_words)
         nc.vector.tensor_copy(xtg_s[:], xt_plane[:].indirect(l1[:]))
-        deal_scales(ws_dealt, 0)
         nc.vector.tensor_copy(xtg_w[:], xt_w[:].indirect(l1[:]))
+        wc_w = tile("wc_w", [P, N], U32, tag="xt_w")
+        nc.scalar.dma_start(wc_w[:].bitcast(I32), words4(wc_words))
 
         acc = [ps.tile([P, 4, H], F32, name="acc%d" % h) for h in range(2)]
         for h in range(2):
@@ -139,7 +145,7 @@ def tile_list_chained_bank_kernel(
         deal_scales(w0s_dealt, 1)
         spread(xo_plane, xo_s_words)
         nc.vector.tensor_copy(xog_s[:], xo_plane[:].indirect(l2[:]))
-        xog_w = tile("xog_w", [P, J], U32, tag="xo_s")
+        xog_w = tile("xog_w", [P, J], U32)
 
         hid = [tile("hid%d" % h, [P, H, 4], BF16) for h in range(2)]
         for h in range(2):
@@ -159,8 +165,9 @@ def tile_list_chained_bank_kernel(
 
         wbc_plane = tile("wbc_plane", [P, 2 * N], U8, tag="xo_w")
         wbc_flat = wbc_s[:].bitcast(I32)
-        nc.vector.tensor_copy(wbc_plane[0:64, :].bitcast(I32), wbc_flat[0:64, 0:128])
-        nc.vector.tensor_copy(wbc_plane[64:128, :].bitcast(I32), wbc_flat[0:64, 128:256])
+        nc.vector.memset(wbc_plane[:].bitcast(I32), 0)
+        for q in range(4):
+            nc.vector.tensor_copy(wbc_plane[32 * q : 32 * q + 4, :].bitcast(I32), wbc_flat[0:4, 128 * q : 128 * (q + 1)])
 
         hq_w = tile("hq_w", [P, J], U32, tag="wbc_s")
         hq_s = tile("hq_s", [P, J], U8)
@@ -181,18 +188,18 @@ def tile_list_chained_bank_kernel(
                     start=True,
                     stop=True,
                 )
-        for n in range(2):
-            nc.tensor.matmul_mx(
-                q_ps[n][:],
-                lhsT=wc_w[:, 128 * n : 128 * (n + 1)].bitcast(E4M3),
-                lhsT_scale=wbc_plane[:, N + 128 * n : N + 128 * (n + 1)],
-                rhs=hq_w[:].bitcast(E4M3),
-                rhs_scale=hq_s[:],
-                start=True,
-                stop=True,
-            )
+            for n in range(2):
+                nc.tensor.matmul_mx(
+                    q_ps[n][:, cols],
+                    lhsT=wc_w[:, 128 * n : 128 * (n + 1)].bitcast(E4M3),
+                    lhsT_scale=wbc_plane[:, N + 128 * n : N + 128 * (n + 1)],
+                    rhs=hq_w[:, cols].bitcast(E4M3),
+                    rhs_scale=hq_s[:, cols],
+                    start=True,
+                    stop=True,
+                )
         p_sb = [
-            [tile("p_sb00", [P, H], F32, tag="hid1"), tile("p_sb01", [P, H], F32)],
+            [tile("p_sb00", [P, H], F32), tile("p_sb01", [P, H], F32)],
             [tile("p_sb10", [P, H], F32), tile("p_sb11", [P, H], F32)],
         ]
         pg = [tile("pg%d" % n, [P, C], F32) for n in range(2)]
@@ -209,7 +216,7 @@ def tile_list_chained_bank_kernel(
         for n in range(2):
             move(n, p_sb[0][n][:], p_ps[0][n][:])
             move(n, pw[n][:].indirect(l3[:, 0:8]), p_sb[0][n][:])
-        q_sb = [tile("q_sb0", [P, J], F32, tag="hid1"), tile("q_sb1", [P, J], F32, tag="p_sb01")]
+        q_sb = [tile("q_sb%d" % n, [P, J], F32) for n in range(2)]
         for n in range(2):
             move(n, p_sb[1][n][:], p_ps[1][n][:])
             move(n, q_sb[n][:], q_ps[n][:])

@@ -57,11 +57,10 @@ def tile_list_chained_bank_kernel(
 
         nc.vector.memset(xt_s[:, 0:T].bitcast(I32), 0)
         nc.gpsimd.memset(xt_s[:, T : 2 * T].bitcast(I32), 0)
-        nc.vector.memset(xo_s[:, 0:Z].bitcast(I32), 0)
-        nc.gpsimd.memset(xo_s[:, Z : 2 * Z].bitcast(I32), 0)
+        nc.vector.memset(xo_s[:].bitcast(I32), 0)
         nc.vector.memset(ws_plane[:].bitcast(I32), 0)
         nc.vector.memset(pw[0][:], 0.0)
-        nc.gpsimd.memset(pw[1][:], 0.0)
+        nc.vector.memset(pw[1][:], 0.0)
 
         def words4(ap):
             return ap[0].rearrange("p n t -> p (n t)").bitcast(I32)
@@ -221,7 +220,6 @@ def tile_list_chained_bank_kernel(
             move(n, p_sb[1][n][:], p_ps[1][n][:])
             move(n, q_sb[n][:], q_ps[n][:])
             move(n, pw[n][:].indirect(l3[:, 8:16]), p_sb[1][n][:])
-            move(n, pick_q[n][:], q_sb[n][:].indirect(l6[:]))
 
         moved = [tile("moved%d" % n, [P, C], F32) for n in range(2)]
 
@@ -231,11 +229,13 @@ def tile_list_chained_bank_kernel(
         def sub(n, c0, c1):
             nc.vector.tensor_tensor(pg[n][:, c0:c1], pw[n][:, c0:c1], moved[n][:, c0:c1], ALU.subtract)
 
+        move(0, pick_q[0][:], q_sb[0][:].indirect(l6[:]))
         fetch(0, 0, 0, 256)
         fetch(1, 0, 256, 512)
         fetch(0, 1, 384, 512)
         fetch(1, 1, 0, 256)
         fetch(1, 1, 256, 384)
+        move(1, pick_q[1][:], q_sb[1][:].indirect(l6[:]))
         sub(0, 0, 512)
         sub(1, 0, 256)
         sub(1, 256, 512)

@@ -55,8 +55,7 @@ def tile_list_chained_bank_kernel(
 
         ws_plane = tile("ws_plane", [P, 2 * R], U8)
 
-        nc.vector.memset(xt_s[:, 0:T].bitcast(I32), 0)
-        nc.gpsimd.memset(xt_s[:, T : 2 * T].bitcast(I32), 0)
+        nc.vector.memset(xt_s[:].bitcast(I32), 0)
         nc.vector.memset(xo_s[:].bitcast(I32), 0)
         nc.vector.memset(ws_plane[:].bitcast(I32), 0)
         nc.vector.memset(pw[0][:], 0.0)
@@ -77,15 +76,15 @@ def tile_list_chained_bank_kernel(
         wbc_words = wbc_s[:].bitcast(I32).rearrange("p (q a n) -> p q a n", q=4, a=2)
 
         nc.sync.dma_start(l1[:], offs)
+        nc.sync.dma_start(l2[:], offs2)
         for a, scales in enumerate((w_scales, w0_scales)):
             nc.scalar.dma_start(ws_words[0:4, :, a, :], rows_q(scales))
         for l in range(2):
             nc.sync.dma_start(xt_s_words[64 + 32 * l : 68 + 32 * l], rows_hl(xt_scales, l))
         nc.scalar.dma_start(w_raw[:].bitcast(I32), w_words[0].bitcast(I32))
-        nc.sync.dma_start(xt_w[:].bitcast(I32), words4(xt_words))
-        nc.scalar.dma_start(xo_s_words[64:68], rows_hl(xo_scales, 0))
-        nc.sync.dma_start(l2[:], offs2)
-        nc.sync.dma_start(xo_s_words[96:100], rows_hl(xo_scales, 1))
+        nc.scalar.dma_start(xt_w[:].bitcast(I32), words4(xt_words))
+        for l in range(2):
+            nc.sync.dma_start(xo_s_words[64 + 32 * l : 68 + 32 * l], rows_hl(xo_scales, l))
         nc.sync.dma_start(w0_raw[:].bitcast(I32), w0_words[0].bitcast(I32))
         nc.sync.dma_start(xo_w[:].bitcast(I32), words4(xo_words))
         for a, scales in enumerate((wb_scales, wc_scales)):
@@ -101,8 +100,6 @@ def tile_list_chained_bank_kernel(
         for dst, src in ((w_dealt, w_raw), (w0_dealt, w0_raw)):
             o_ap, i_ap = deal(dst[:].bitcast(U16), src[:].bitcast(U16), 8)
             nc.scalar.copy(o_ap, i_ap)
-        wb_w = tile("wb_w", [P, 2 * N], U8, tag="w_raw")
-        nc.scalar.dma_start(wb_w[:].bitcast(I32), wb_words[0].bitcast(I32))
 
         def spread(plane, staged):
             nc.vector.tensor_copy(plane[0:64, :].bitcast(I32), staged[64:128, 0, :])
@@ -124,6 +121,8 @@ def tile_list_chained_bank_kernel(
         deal_scales(ws_dealt, 0)
         spread(xt_plane, xt_s_words)
         nc.vector.tensor_copy(xtg_s[:], xt_plane[:].indirect(l1[:]))
+        wb_w = tile("wb_w", [P, 2 * N], U8, tag="xt_plane")
+        nc.scalar.dma_start(wb_w[:].bitcast(I32), wb_words[0].bitcast(I32))
         nc.vector.tensor_copy(xtg_w[:], xt_w[:].indirect(l1[:]))
         wc_w = tile("wc_w", [P, N], U32, tag="xt_w")
         nc.scalar.dma_start(wc_w[:].bitcast(I32), words4(wc_words))

from contextlib import ExitStack

import concourse.mybir as mybir

K, F, T, Z, J, R, N, C, O = 512, 512, 1024, 1024, 256, 512, 256, 512, 128
FLOPS = 2 * (K * R * J + F * R * J + 2 * R * N * J)

F32 = mybir.dt.float32
BF16 = mybir.dt.bfloat16
I32 = mybir.dt.int32
U32 = mybir.dt.uint32
U16 = mybir.dt.uint16
U8 = mybir.dt.uint8
E4M3 = mybir.dt.float8_e4m3fn_x4
E5M2 = mybir.dt.float8_e5m2_x4
E2M1 = mybir.dt.float4_e2m1fn_x4
ACT = mybir.ActivationFunctionType
ALU = mybir.AluOpType

P = 128
H = 128


def tile_list_chained_bank_kernel(
    tc, xt_words, xt_scales, w_words, w_scales, xo_words, xo_scales, w0_words, w0_scales,
    wb_words, wb_scales, wc_words, wc_scales, offs, offs2, offs3, offs4, offs5, offs6, out,
):
    nc = tc.nc
    with ExitStack() as ctx:
        sb = ctx.enter_context(tc.tile_pool(name="sb", bufs=1))
        ps = ctx.enter_context(tc.psum_pool(name="ps", bufs=1))

        def tile(name, shape, dtype, tag=None):
            return sb.tile(shape, dtype, name=name, tag=tag or name, align_bytes=64)

        l1 = tile("l1", [P, 16], U16)
        l2 = tile("l2", [P, 16], U16)
        l3 = tile("l3", [P, 16], U16)
        l4 = tile("l4", [P, 32], U16)
        l5 = tile("l5", [P, 8], U16)
        l6 = tile("l6", [P, 8], U16)
        xt_w = tile("xt_w", [P, T], U32)
        xo_w = tile("xo_w", [P, Z], U32)
        xt_s = tile("xt_s", [P, 2 * T], U8)
        xo_s = tile("xo_s", [P, 2 * Z], U8)
        w_raw = tile("w_raw", [P, 2 * R], U8)
        w0_raw = tile("w0_raw", [P, 2 * R], U8)
        w_dealt = tile("w_dealt", [P, 2 * R], U8)
        w0_dealt = tile("w0_dealt", [P, 2 * R], U8)
        ws_raw = tile("ws_raw", [P, 4 * 2 * R], U8)
        ws_dealt = tile("ws_dealt", [P, R], U8)
        w0s_dealt = tile("w0s_dealt", [P, R], U8)
        wbc_s = tile("wbc_s", [P, 4 * 2 * N], U8)
        pw = [tile("pw%d" % n, [P, C], F32) for n in range(2)]

        ws_plane = tile("ws_plane", [P, 2 * R], U8)

        nc.vector.memset(xt_s[:].bitcast(I32), 0)
        nc.vector.memset(xo_s[:].bitcast(I32), 0)
        nc.vector.memset(ws_plane[:].bitcast(I32), 0)
        nc.vector.memset(pw[0][:], 0.0)
        nc.vector.memset(pw[1][:], 0.0)

        def words4(ap):
            return ap[0].rearrange("p n t -> p (n t)").bitcast(I32)

        def rows_q(ap):
            return ap[0].bitcast(I32).rearrange("(q r) n -> r q n", r=4)

        def rows_hl(ap, l):
            return ap[0].bitcast(I32).rearrange("(h l r) n -> l r h n", h=2, l=2)[l]

        ws_words = ws_raw[:].bitcast(I32).rearrange("p (q a n) -> p q a n", q=4, a=2)
        xt_s_words = xt_s[:].bitcast(I32).rearrange("p (h n) -> p h n", h=2)
        xo_s_words = xo_s[:].bitcast(I32).rearrange("p (h n) -> p h n", h=2)
        wbc_words = wbc_s[:].bitcast(I32).rearrange("p (q a n) -> p q a n", q=4, a=2)

        nc.sync.dma_start(l1[:], offs)
        nc.sync.dma_start(l2[:], offs2)
        for a, scales in enumerate((w_scales, w0_scales)):
            nc.scalar.dma_start(ws_words[0:4, :, a, :], rows_q(scales))
        for l in range(2):
            nc.sync.dma_start(xt_s_words[64 + 32 * l : 68 + 32 * l], rows_hl(xt_scales, l))
        nc.scalar.dma_start(w_raw[:].bitcast(I32), w_words[0].bitcast(I32))
        nc.scalar.dma_start(xt_w[:].bitcast(I32), words4(xt_words))
        for l in range(2):
            nc.sync.dma_start(xo_s_words[64 + 32 * l : 68 + 32 * l], rows_hl(xo_scales, l))
        nc.sync.dma_start(w0_raw[:].bitcast(I32), w0_words[0].bitcast(I32))
        nc.sync.dma_start(xo_w[:].bitcast(I32), words4(xo_words))
        for a, scales in enumerate((wb_scales, wc_scales)):
            nc.sync.dma_start(wbc_words[0:4, :, a, :], rows_q(scales))
        nc.sync.dma_start(l3[:], offs3)
        nc.sync.dma_start(l6[:], offs6)
        nc.sync.dma_start(l4[:], offs4)
        nc.sync.dma_start(l5[:], offs5)

        def deal(dst, src, run):
            return (dst.rearrange("p (t c i) -> p c t i", t=4, i=run), src.rearrange("p (c i t) -> p c t i", t=4, i=run))

        for dst, src in ((w_dealt, w_raw), (w0_dealt, w0_raw)):
            o_ap, i_ap = deal(dst[:].bitcast(U16), src[:].bitcast(U16), 8)
            nc.scalar.copy(o_ap, i_ap)

        def spread(plane, staged):
            nc.vector.tensor_copy(plane[0:64, :].bitcast(I32), staged[64:128, 0, :])
            nc.vector.tensor_copy(plane[64:128, :].bitcast(I32), staged[64:128, 1, :])

        def deal_scales(dst, a):
            o_ap, i_ap = deal(dst[:], ws_plane[:, a * R : (a + 1) * R], 16)
            nc.vector.tensor_copy(o_ap, i_ap)

        xt_plane = tile("xt_plane", [P, T], U8)
        xo_plane = tile("xo_plane", [P, Z], U8)
        xtg_w = tile("xtg_w", [P, J], U32)
        xtg_s = tile("xtg_s", [P, J], U8)
        xog_s = tile("xog_s", [P, J], U8)
        ws_flat = ws_raw[:].bitcast(I32)
        quarter = 2 * R // 4
        for q in range(4):
            nc.vector.tensor_copy(ws_plane[32 * q : 32 * q + 4, :].bitcast(I32), ws_flat[0:4, q * quarter : (q + 1) * quarter])
        deal_scales(ws_dealt, 0)
        spread(xt_plane, xt_s_words)
        nc.vector.tensor_copy(xtg_s[:], xt_plane[:].indirect(l1[:]))
        wb_w = tile("wb_w", [P, 2 * N], U8, tag="xt_plane")
        nc.scalar.dma_start(wb_w[:].bitcast(I32), wb_words[0].bitcast(I32))
        nc.vector.tensor_copy(xtg_w[:], xt_w[:].indirect(l1[:]))
        wc_w = tile("wc_w", [P, N], U32, tag="xt_w")
        nc.scalar.dma_start(wc_w[:].bitcast(I32), words4(wc_words))

        acc = [ps.tile([P, 4, H], F32, name="acc%d" % h) for h in range(2)]
        for h in range(2):
            for t in range(4):
                nc.tensor.matmul_mx(
                    acc[h][:, t, :],
                    lhsT=w_dealt[:, 256 * t : 256 * (t + 1)].bitcast(E2M1),
                    lhsT_scale=ws_dealt[:, 128 * t : 128 * (t + 1)],
                    rhs=xtg_w[:, H * h : H * (h + 1)].bitcast(E5M2),
                    rhs_scale=xtg_s[:, H * h : H * (h + 1)],
                    start=(t == 0),
                    stop=False,
                )

        deal_scales(w0s_dealt, 1)
        spread(xo_plane, xo_s_words)
        nc.vector.tensor_copy(xog_s[:], xo_plane[:].indirect(l2[:]))
        xog_w = tile("xog_w", [P, J], U32)

        hid = [tile("hid%d" % h, [P, H, 4], BF16) for h in range(2)]
        for h in range(2):
            nc.vector.tensor_copy(xog_w[:, H * h : H * (h + 1)], xo_w[:].indirect(l2[:, 8 * h : 8 * (h + 1)]))
        for h in range(2):
            for t in range(4):
                nc.tensor.matmul_mx(
                    acc[h][:, t, :],
                    lhsT=w0_dealt[:, 256 * t : 256 * (t + 1)].bitcast(E2M1),
                    lhsT_scale=w0s_dealt[:, 128 * t : 128 * (t + 1)],
                    rhs=xog_w[:, H * h : H * (h + 1)].bitcast(E4M3),
                    rhs_scale=xog_s[:, H * h : H * (h + 1)],
                    start=False,
                    stop=(t == 3),
                )
            nc.scalar.activation(hid[h][:], acc[h][:].rearrange("p t j -> p j t"), ACT.Relu)

        wbc_plane = tile("wbc_plane", [P, 2 * N], U8, tag="xo_w")
        wbc_flat = wbc_s[:].bitcast(I32)
        nc.vector.memset(wbc_plane[:].bitcast(I32), 0)
        for q in range(4):
            nc.vector.tensor_copy(wbc_plane[32 * q : 32 * q + 4, :].bitcast(I32), wbc_flat[0:4, 128 * q : 128 * (q + 1)])

        hq_w = tile("hq_w", [P, J], U32, tag="wbc_s")
        hq_s = tile("hq_s", [P, J], U8)
        p_ps = [[ps.tile([P, H], F32, name="p_ps%d%d" % (h, n)) for n in range(2)] for h in range(2)]
        q_ps = [ps.tile([P, J], F32, name="q_ps%d" % n) for n in range(2)]
        for h in range(2):
            cols = slice(H * h, H * (h + 1))
            nc.vector.quantize_mx(
                out=hq_w[:, cols].bitcast(E4M3), scales=hq_s[:, cols], in_=hid[h][:].rearrange("p j t -> p (j t)")
            )
            for n in range(2):
                nc.tensor.matmul_mx(
                    p_ps[h][n][:],
                    lhsT=wb_w[:, 256 * n : 256 * (n + 1)].bitcast(E2M1),
                    lhsT_scale=wbc_plane[:, 128 * n : 128 * (n + 1)],
                    rhs=hq_w[:, cols].bitcast(E4M3),
                    rhs_scale=hq_s[:, cols],
                    start=True,
                    stop=True,
                )
            for n in range(2):
                nc.tensor.matmul_mx(
                    q_ps[n][:, cols],
                    lhsT=wc_w[:, 128 * n : 128 * (n + 1)].bitcast(E4M3),
                    lhsT_scale=wbc_plane[:, N + 128 * n : N + 128 * (n + 1)],
                    rhs=hq_w[:, cols].bitcast(E4M3),
                    rhs_scale=hq_s[:, cols],
                    start=True,
                    stop=True,
                )
        p_sb = [
            [tile("p_sb00", [P, H], F32), tile("p_sb01", [P, H], F32)],
            [tile("p_sb10", [P, H], F32), tile("p_sb11", [P, H], F32)],
        ]
        pg = [tile("pg%d" % n, [P, C], F32) for n in range(2)]
        pick_p = [tile("pick_p%d" % n, [P, O], F32) for n in range(2)]
        pick_q = [tile("pick_q%d" % n, [P, O], F32) for n in range(2)]
        y = [tile("y%d" % n, [P, O], F32) for n in range(2)]

        def move(n, dst, src):
            if n == 0:
                nc.vector.tensor_copy(dst, src)
            else:
                nc.scalar.activation(dst, src, ACT.Copy)

        for n in range(2):
            move(n, p_sb[0][n][:], p_ps[0][n][:])
            move(n, pw[n][:].indirect(l3[:, 0:8]), p_sb[0][n][:])
        q_sb = [tile("q_sb%d" % n, [P, J], F32) for n in range(2)]
        for n in range(2):
            move(n, p_sb[1][n][:], p_ps[1][n][:])
            move(n, q_sb[n][:], q_ps[n][:])
            move(n, pw[n][:].indirect(l3[:, 8:16]), p_sb[1][n][:])

        moved = [tile("moved%d" % n, [P, C], F32) for n in range(2)]

        def fetch(engine, n, c0, c1):
            move(engine, moved[n][:, c0:c1], pw[n][:].indirect(l4[:, c0 // 16 : c1 // 16]))

        def sub(n, c0, c1):
            nc.vector.tensor_tensor(pg[n][:, c0:c1], pw[n][:, c0:c1], moved[n][:, c0:c1], ALU.subtract)

        move(0, pick_q[0][:], q_sb[0][:].indirect(l6[:]))
        fetch(0, 0, 0, 256)
        fetch(1, 0, 256, 512)
        fetch(0, 1, 384, 512)
        fetch(1, 1, 0, 256)
        fetch(1, 1, 256, 384)
        move(1, pick_q[1][:], q_sb[1][:].indirect(l6[:]))
        sub(0, 0, 512)
        sub(1, 0, 256)
        sub(1, 256, 512)
        for n in range(2):
            move(1, pick_p[n][:], pg[n][:].indirect(l5[:]))
            nc.vector.tensor_tensor(y[n][:], pick_p[n][:], pick_q[n][:], ALU.max)
            nc.sync.dma_start(out[n * P : (n + 1) * P, :], y[n][:])
